import numpy as np, ml_dtypes
CORES = [21,29,37,45,53,61,69,77,85]
N = 9
WB, KB, QP = 1, 4, 64
def setup_inputs(rng):
    return {"q": rng.standard_normal((N, 128, QP), dtype=np.float32).astype(ml_dtypes.bfloat16), "k": rng.standard_normal((N, 128, KB * 128), dtype=np.float32).astype(ml_dtypes.bfloat16), "v": rng.standard_normal((N, 128, KB * 128), dtype=np.float32).astype(ml_dtypes.bfloat16)}
def setup_inputs_big(rng):
    d = setup_inputs(rng)
    for k in ("q", "k", "v"): d[k] = (d[k].astype(np.float32) * 1024.0).astype(d[k].dtype)
    return d
def setup_inputs_small(rng):
    d = setup_inputs(rng)
    for k in ("q", "k", "v"): d[k] = (d[k].astype(np.float32) * (1 / 1024.0)).astype(d[k].dtype)
    return d
def setup_inputs_apart(rng):
    d = setup_inputs(rng)
    f = (10.0 ** rng.permutation(np.linspace(-1.5, 1.5, N))).astype(np.float32).reshape(N, 1, 1)
    for k in ("q", "k", "v"): d[k] = (d[k].astype(np.float32) * f).astype(d[k].dtype)
    return d
def reference(q, k, v):
    Q, K, V = q.astype(np.float64), k.astype(np.float64), v.astype(np.float64)
    y = np.zeros((N, 128, QP))
    for r in range(N):
        for j in range(max(0, r - WB), r + 1):
            for b in range(KB):
                S = np.maximum(K[j][:, 128 * b:128 * b + 128].T @ Q[r], 0.0)
                y[r] += V[j][:, 128 * b:128 * b + 128].T @ S
    return {"y": y.astype(ml_dtypes.bfloat16 if q.dtype != np.float64 else np.float64)}

from concourse.mybir import AluOpType

KB = 4
BW = 128
QP = 64

SCRATCH = {
    "qd": ("dram", [128, QP], "bfloat16"),
    "qsb": ("sbuf", [128, QP], "bfloat16"),
    "kv": ("sbuf", [128, 2 * KB * BW], "bfloat16"),
    "zero": ("sbuf", [128, QP], "float32"),
    "p": ("sbuf", [128, KB * QP], "bfloat16"),
    "osb": ("sbuf", [128, QP], "bfloat16"),
    "land": ("sbuf", [128, QP], "bfloat16"),
    "s0": ("psum", [128, 512], "float32"),
    "s1": ("psum", [128, 512], "float32"),
    "s2": ("psum", [128, 512], "float32"),
    "s3": ("psum", [128, 512], "float32"),
    "o": ("psum", [128, 512], "float32"),
}
SEMAPHORES = ["qst", "qld", "kvld", "qarr", "kvarr", "larr", "sent", "zs", "om", "ordy", "yst",
              "sm0", "sm1", "sm2", "sm3", "rl0", "rl1", "rl2", "rl3"]


def _helpers(T, topo):
    cores = list(T.cores)
    n = len(cores)
    out = []
    for r, c in enumerate(cores):
        pick = None
        for x in range(topo.CHIPS * topo.CORES_PER_CHIP):
            if x in cores or topo.chip(x) != topo.chip(c) or topo.die(x) != topo.die(c):
                continue
            if not topo.may_write(c, x):
                continue
            if r > 0 and not topo.may_write(x, out[r - 1]):
                continue
            if r < n - 1 and not topo.may_write(x, cores[r + 1]):
                continue
            pick = x
            break
        out.append(pick)
    return out


def _engines(topo, src, dst, want):
    m = topo.mask(src, dst)
    bits = [b for b in range(16) if (m >> b) & 1]
    n = min(want, len(bits))
    chosen = bits[::len(bits) // n][:n]
    mask = 0
    for b in chosen:
        mask |= 1 << b
    return mask, n


def _write(g, T, topo, src, dst, out_ap, in_ap, remote_sem, want):
    rid, pid, _ = topo.addr(dst)
    mask, n = _engines(topo, src, dst, want)
    g.remote_dma(out_ap=out_ap, in_ap=in_ap, remote_sem=remote_sem, local_sem=T.sem.sent,
                 pid=pid, routing_id=rid, dma_engine_mask=mask)
    return n


def _attend(g, T, waits):
    te, ve = g.tensor, g.vector
    ve.memset(T.zero[:], 0.0).then_inc(T.sem.zs, 1)
    ve.wait_ge(T.sem.zs, 1)
    for sem, val in waits:
        te.wait_ge(sem, val)
    for b in range(KB):
        te.matmul(T["s%d" % b][:, 0:QP], T.kv[:, b * BW:(b + 1) * BW], T.qsb[:], True, True).then_inc(
            T.sem["sm%d" % b], 1)
    for b in range(KB):
        ve.wait_ge(T.sem["sm%d" % b], 1)
        ve.tensor_tensor(T.p[:, b * QP:(b + 1) * QP], T["s%d" % b][:, 0:QP], T.zero[:], AluOpType.max).then_inc(
            T.sem["rl%d" % b], 1)
    for b in range(KB):
        te.wait_ge(T.sem["rl%d" % b], 1)
        mm = te.matmul(T.o[:, 0:QP], T.kv[:, (KB + b) * BW:(KB + b + 1) * BW], T.p[:, b * QP:(b + 1) * QP],
                       b == 0, b == KB - 1)
        if b == KB - 1:
            mm.then_inc(T.sem.om, 1)
    ve.wait_ge(T.sem.om, 1)


Q_ENG = 4
KV_ENG = 16
OFF_ENG = 8


def rank_program(g, core, T, topo):
    cores = list(T.cores)
    n = len(cores)
    helpers = _helpers(T, topo)
    rank = T.rank_of(core)
    half = KB * BW

    if rank is not None:
        x = helpers[rank]
        sends_q = rank > 0
        sends_kv = rank < n - 1
        if sends_q:
            g.sync.dma_start(T.qd[:], T.q[:]).then_inc(T.sem.qst, 16)
        g.sync.dma_start(T.kv[:, 0:half], T.k[:]).then_inc(T.sem.kvld, 16)
        g.scalar.dma_start(T.kv[:, half:2 * half], T.v[:]).then_inc(T.sem.kvld, 16)
        g.scalar.dma_start(T.qsb[:], T.q[:]).then_inc(T.sem.qld, 16)
        sent = 0
        if sends_q:
            g.wait_ge(T.sem.qst, 16)
            sent += _write(g, T, topo, core, x, T.qd[:], T.qd[:], T.sem.qarr, Q_ENG)
        if sends_kv:
            g.wait_ge(T.sem.kvld, 32)
            sent += _write(g, T, topo, core, x, T.kv[:], T.kv[:], T.sem.kvarr, KV_ENG)
        _attend(g, T, [(T.sem.kvld, 32), (T.sem.qld, 16)])
        if sends_q:
            _, n_off = _engines(topo, helpers[rank - 1], core, OFF_ENG)
            g.vector.wait_ge(T.sem.larr, n_off)
            g.vector.tensor_tensor(T.osb[:], T.o[:, 0:QP], T.land[:], AluOpType.add).then_inc(T.sem.ordy, 1)
        else:
            g.vector.tensor_copy(T.osb[:], T.o[:, 0:QP]).then_inc(T.sem.ordy, 1)
        g.sync.wait_ge(T.sem.ordy, 1)
        g.sync.dma_start(T.y[:], T.osb[:]).then_inc(T.sem.yst, 16)
        g.sync.wait_ge(T.sem.yst, 16)
        if sent:
            g.wait_ge(T.sem.sent, sent)
        return

    if core not in helpers:
        return
    r = helpers.index(core)
    passes_q = r > 0
    computes = r < n - 1
    sent = 0
    if passes_q:
        _, n_q = _engines(topo, cores[r], core, Q_ENG)
        g.wait_ge(T.sem.qarr, n_q)
        sent += _write(g, T, topo, core, helpers[r - 1], T.qsb[:], T.qd[:], T.sem.qld, OFF_ENG)
    if computes:
        _, n_kv = _engines(topo, cores[r], core, KV_ENG)
        _, n_qn = _engines(topo, helpers[r + 1], core, OFF_ENG)
        _attend(g, T, [(T.sem.kvarr, n_kv), (T.sem.qld, n_qn)])
        g.vector.tensor_copy(T.osb[:], T.o[:, 0:QP]).then_inc(T.sem.ordy, 1)
        g.wait_ge(T.sem.ordy, 1)
        sent += _write(g, T, topo, core, cores[r + 1], T.land[:], T.osb[:], T.sem.larr, OFF_ENG)
    if sent:
        g.wait_ge(T.sem.sent, sent)
